import numpy as np
import ml_dtypes


def mxq(x, axis, fmt="e4m3"):
    dtype, down = {"e4m3": (ml_dtypes.float8_e4m3fn, 7), "e5m2": (ml_dtypes.float8_e5m2, 14)}[fmt]
    v = np.moveaxis(np.asarray(x, np.float32).astype(ml_dtypes.bfloat16).astype(np.float64), axis, -1)
    blocks = v.reshape(v.shape[:-1] + (-1, 32))
    amax = np.abs(blocks).max(-1, keepdims=True)
    byte = np.maximum(np.where(amax > 0, np.frexp(amax)[1] - 1 + 127, 0) - down, 1)
    scale = np.exp2(byte - 127.0)
    codes = (blocks / scale).astype(np.float32).astype(dtype).astype(np.float64)
    return np.moveaxis((codes * scale).reshape(v.shape), -1, axis)


WIDE = False


def mx_kscale(k):
    if not WIDE:
        return np.ones(k)
    levels = np.array([10, -10, 5, -5, 0])
    if k % 512:
        return np.exp2(np.random.permutation(np.resize(levels, k // 32))).repeat(32)
    a = np.empty((k // 512, 16))
    for p in range(k // 512):
        a[p, :8] = np.random.permutation(np.resize(levels, 8))
        for g in range(8):
            far = levels[np.abs(levels - a[p, g]) >= 10]
            a[p, g + 8] = far[np.random.randint(len(far))]
    return np.exp2(a.ravel()).repeat(32)


def f64(x):
    return np.asarray(x).astype(np.float64)


def striped(idx):
    return np.tile(idx.reshape(-1, 16).T, (8, 1)).astype(np.uint16)


def unstriped(offs):
    return offs[:16].T.reshape(-1).astype(np.int64)


def pack_weight(w):
    k, n = w.shape
    w = f64(np.asarray(w, np.float32).astype(ml_dtypes.bfloat16)).reshape(k // 32, 32, n)
    amax = np.abs(w).max(1)
    byte = np.clip(np.where(amax > 0, np.frexp(amax)[1] - 1 + 127 - 7, 1), 1, 254)
    scaled = (w * np.exp2(127.0 - byte)[:, None, :]).reshape(k, n).astype(np.float32)
    words = np.ascontiguousarray(scaled.reshape(k // 512, 128, 4, n).transpose(0, 1, 3, 2)).astype(ml_dtypes.float8_e4m3fn).view(np.uint8)
    return words, np.ascontiguousarray(byte.astype(np.uint8).reshape(k // 512, 16, n))


def unpack_weight(words, scales):
    g, p, n, _ = words.shape
    vals = np.ascontiguousarray(words).view(ml_dtypes.float8_e4m3fn).astype(np.float64) * np.repeat(np.exp2(scales.astype(np.float64) - 127.0), 8, axis=1)[..., None]
    return vals.transpose(0, 1, 3, 2).reshape(g * 512, n)


E2M1 = np.array([0.0, 0.5, 1.0, 1.5, 2.0, 3.0, 4.0, 6.0, -0.0, -0.5, -1.0, -1.5, -2.0, -3.0, -4.0, -6.0])


def pack_fp4(w):
    k, n = w.shape
    w = f64(np.asarray(w, np.float32).astype(ml_dtypes.bfloat16)).reshape(k // 32, 32, n)
    amax = np.abs(w).max(1)
    mant, ex = np.frexp(amax / 6.0)
    byte = np.clip(np.where(amax > 0, np.where(mant > 0.5, ex, ex - 1) + 127, 1), 1, 254)
    scaled = (w * np.exp2(127.0 - byte)[:, None, :]).reshape(k, n).astype(np.float32)
    c = np.ascontiguousarray(scaled.reshape(k // 512, 128, 4, n).transpose(0, 1, 3, 2)).astype(ml_dtypes.float4_e2m1fn).view(np.uint8) & 0xF
    words = (c[..., 0::2] | (c[..., 1::2] << 4)).reshape(k // 512, 128, 2 * n)
    return np.ascontiguousarray(words), np.ascontiguousarray(byte.astype(np.uint8).reshape(k // 512, 16, n))


def unpack_fp4(words, scales):
    g, _, n = scales.shape
    words = np.ascontiguousarray(words).reshape(g, 128, n, 2)
    nib = np.empty((g, 128, n, 4), np.uint8)
    nib[..., 0::2] = words & 0xF
    nib[..., 1::2] = words >> 4
    vals = E2M1[nib] * np.repeat(np.exp2(scales.astype(np.float64) - 127.0), 8, axis=1)[..., None]
    return vals.transpose(0, 1, 3, 2).reshape(g * 512, n)


K, T, S, N, H, V, U = 512, 1024, 512, 256, 512, 256, 512


def setup_inputs():
    n = np.random.standard_normal
    s = mx_kscale(K)[:, None]
    u = mx_kscale(H)
    packed_xT = pack_weight(n((K, T)) * s)
    packed_w1 = pack_fp4(n((K, H)) / np.sqrt(K) / s)
    packed_w2 = pack_fp4(n((H, N)) / np.sqrt(H) / u[:, None])
    return {
        "x_words": packed_xT[0],
        "x_scales": packed_xT[1],
        "w1_words": packed_w1[0],
        "w1_scales": packed_w1[1],
        "sza": (np.random.uniform(1.0, 3.0, (H, V))).astype(np.float32),
        "szb": (np.random.uniform(1.0, 3.0, (H, V))).astype(np.float32),
        "unit": (np.random.uniform(0.6, 1.4, (H, 1)) * u[:, None]).astype(np.float32),
        "w2_words": packed_w2[0],
        "w2_scales": packed_w2[1],
        "skip": (n((N, U))).astype(np.float32),
        "offs": striped(np.random.permutation(T)[:S]),
        "dst": striped(np.random.permutation(S)[:V]),
        "src": striped(np.random.permutation(S)[:V]),
        "own": striped(np.random.permutation(np.concatenate([np.arange(V), np.random.randint(0, V, U - V)]))),
    }


def reference(x_words, x_scales, w1_words, w1_scales, sza, szb, unit, w2_words, w2_scales, skip, offs, dst, src, own):
    xq = unpack_weight(x_words, x_scales)[:, unstriped(offs)]
    y = unpack_fp4(w1_words, w1_scales).T @ xq
    yd = y[:, unstriped(dst)]
    yr = y[:, unstriped(src)]
    sz = f64(sza) + f64(szb)
    mrg = (yd * f64(sza) + yr * f64(szb)) / sz
    ty = np.tanh(y)
    hm = mrg * ty[:, unstriped(src)]
    un = hm[:, unstriped(own)]
    hid = f64(unit) * un
    rr = unpack_fp4(w2_words, w2_scales).T @ mxq(hid, 0, "e4m3")
    return rr + f64(skip)

@@ -1,0 +1,180 @@
+from contextlib import ExitStack
+
+import concourse.mybir as mybir
+
+F32 = mybir.dt.float32
+BF16 = mybir.dt.bfloat16
+I32 = mybir.dt.int32
+U32 = mybir.dt.uint32
+U16 = mybir.dt.uint16
+U8 = mybir.dt.uint8
+FP8X4 = mybir.dt.float8_e4m3fn_x4
+FP4X4 = mybir.dt.float4_e2m1fn_x4
+ALU = mybir.AluOpType
+ACT = mybir.ActivationFunctionType
+
+P = 128
+PACK = 4
+T, S, N, H, V, U = 1024, 512, 256, 512, 256, 512
+HALF = S // 2
+CHUNK = 128
+WIDE = 704
+
+FLOPS = 2 * 512 * H * S + 2 * H * N * U
+
+
+def tile_picked_ytomeg_mul_p_kernel(
+    tc, x_words, x_scales, w1_words, w1_scales, sza, szb, unit, w2_words, w2_scales, skip, offs, dst, src, own, out
+):
+    nc = tc.nc
+    with ExitStack() as ctx:
+        keep = ctx.enter_context(tc.tile_pool(name="keep", bufs=1))
+        psum = ctx.enter_context(tc.psum_pool(name="psum", bufs=1))
+
+        def sb(name, shape, dtype):
+            return keep.tile(shape, dtype, name=name, align_bytes=64)
+
+        offs_sb = sb("offs_sb", [P, S // 16], U16)
+        dst_sb = sb("dst_sb", [P, V // 16], U16)
+        src_sb = sb("src_sb", [P, V // 16], U16)
+        own_sb = sb("own_sb", [P, U // 16], U16)
+        xw = sb("xw", [P, T], U32)
+        xs = sb("xs", [P, T], U8)
+        w1w = sb("w1w", [P, 2 * H], U8)
+        w1s = sb("w1s", [P, H], U8)
+        w2w = sb("w2w", [P, 2 * N], U8)
+        w2s = sb("w2s", [P, N], U8)
+        sza_sb = sb("sza_sb", [P, PACK * V], F32)
+        szb_sb = sb("szb_sb", [P, PACK * V], F32)
+        unit_sb = sb("unit_sb", [P, PACK], F32)
+        skip_sb = sb("skip_sb", [P, N // P, U], F32)
+
+        def load_scales(plane, rows, queues):
+            for q in range(4):
+                queues[q].dma_start(
+                    plane[32 * q : 32 * q + 4, :].bitcast(I32), rows[0, 4 * q : 4 * q + 4, :].bitcast(I32)
+                )
+
+        nc.vector.memset(xs[:].bitcast(I32), 0)
+        nc.vector.memset(w1s[:].bitcast(I32), 0)
+        nc.vector.memset(w2s[:].bitcast(I32), 0)
+        nc.sync.dma_start(offs_sb[:], offs)
+        nc.scalar.dma_start(xw[:].bitcast(I32), x_words[0].rearrange("p n t -> p (n t)").bitcast(I32))
+        nc.gpsimd.dma_start(sza_sb[:], sza.rearrange("(p t) v -> p (t v)", t=PACK))
+        nc.gpsimd.dma_start(szb_sb[:], szb.rearrange("(p t) v -> p (t v)", t=PACK))
+        load_scales(xs, x_scales, [nc.sync, nc.scalar, nc.sync, nc.scalar])
+        nc.sync.dma_start(w1w[:].bitcast(I32), w1_words[0].bitcast(I32))
+        load_scales(w1s, w1_scales, [nc.scalar, nc.sync, nc.sync, nc.sync])
+        nc.sync.dma_start(src_sb[:], src)
+        nc.sync.dma_start(dst_sb[:], dst)
+        nc.sync.dma_start(unit_sb[:], unit.rearrange("(p t) o -> p (t o)", t=PACK))
+        nc.sync.dma_start(own_sb[:], own)
+        nc.sync.dma_start(w2w[:].bitcast(I32), w2_words[0].bitcast(I32))
+        load_scales(w2s, w2_scales, [nc.sync] * 4)
+        nc.sync.dma_start(skip_sb[:], skip.rearrange("(h p) c -> p h c", p=P))
+
+        warm = sb("warm", [P, 2], F32)
+        nc.gpsimd.memset(warm[:, 0:1], 1.0)
+        nc.scalar.activation(warm[:, 1:2], warm[:, 0:1], ACT.Abs_reciprocal_sqrt)
+
+        hm = [sb("hm%d" % t, [P, WIDE if t < PACK - 1 else V], F32) for t in range(PACK)]
+        for t in range(PACK - 1):
+            nc.gpsimd.memset(hm[t][:, V:], 0.0)
+
+        w1wd = sb("w1wd", [P, 2 * H], U8)
+        w1sd = sb("w1sd", [P, H], U8)
+        nc.vector.tensor_copy(
+            w1wd[:].rearrange("p (t m b) -> p t m b", t=PACK, b=2),
+            w1w[:].rearrange("p (m t b) -> p t m b", t=PACK, b=2),
+        )
+
+        xqw = [sb("xqw%d" % h, [P, HALF], U32) for h in range(2)]
+        xqs = [sb("xqs%d" % h, [P, HALF], U8) for h in range(2)]
+        y = [sb("y%d" % t, [P, S], F32) for t in range(PACK)]
+        for h in range(2):
+            piece = offs_sb[:, h * (HALF // 16) : (h + 1) * (HALF // 16)]
+            nc.vector.tensor_copy(xqs[h][:], xs[:].indirect(piece))
+            if h == 0:
+                nc.gpsimd.tensor_copy(
+                    w1sd[:].rearrange("p (t m) -> p t m", t=PACK), w1s[:].rearrange("p (m t) -> p t m", t=PACK)
+                )
+            nc.vector.tensor_copy(xqw[h][:], xw[:].indirect(piece))
+            for t in range(PACK):
+                acc = psum.tile([P, HALF], F32, name="y_ps%d_%d" % (h, t), tag="bank%d" % (PACK * h + t))
+                nc.tensor.matmul_mx(
+                    acc[:],
+                    lhsT=w1wd[:, 2 * P * t : 2 * P * (t + 1)].bitcast(FP4X4),
+                    lhsT_scale=w1sd[:, P * t : P * (t + 1)],
+                    rhs=xqw[h][:].bitcast(FP8X4),
+                    rhs_scale=xqs[h][:],
+                    start=True,
+                    stop=True,
+                )
+                nc.scalar.copy(y[t][:, h * HALF : (h + 1) * HALF], acc[:])
+
+        sz = sb("sz", [P, PACK * V], F32)
+        root = sb("root", [P, PACK * V], F32)
+        inv = sb("inv", [P, PACK * V], F32)
+        sgn = sb("sgn", [P, PACK * V], F32)
+        rcp = sb("rcp", [P, PACK * V], F32)
+        pairs = [slice(0, 2 * V), slice(2 * V, 4 * V)]
+        nc.vector.tensor_tensor(sz[:], sza_sb[:], szb_sb[:], ALU.add)
+        nc.scalar.activation(root[:], sz[:], ACT.Abs_reciprocal_sqrt)
+        nc.scalar.activation(inv[:], root[:], ACT.Square)
+        nc.scalar.activation(sgn[:], sz[:], ACT.Sign)
+
+        yr = sb("yr", [P, PACK * V], F32)
+        kept = sb("kept", [P, PACK * V], F32)
+        merged = sb("merged", [P, PACK * V], F32)
+        th = sb("th", [P, PACK * V], F32)
+        both = sb("both", [P, PACK * V], F32)
+        gain = sb("gain", [P, PACK * V], F32)
+        planes = [slice(t * V, (t + 1) * V) for t in range(PACK)]
+        for t in range(PACK):
+            nc.vector.tensor_copy(yr[:, planes[t]], y[t][:].indirect(src_sb[:]))
+        for t in range(PACK):
+            nc.vector.tensor_tensor(kept[:, planes[t]], y[t][:].indirect(dst_sb[:]), sza_sb[:, planes[t]], ALU.mult)
+        nc.scalar.activation(th[:], yr[:], ACT.Tanh)
+        nc.vector.tensor_tensor(merged[:], yr[:], szb_sb[:], ALU.mult)
+        nc.vector.tensor_tensor(rcp[:], inv[:], sgn[:], ALU.mult)
+        nc.vector.tensor_tensor(both[:], kept[:], merged[:], ALU.add)
+        nc.vector.tensor_tensor(gain[:], th[:], rcp[:], ALU.mult)
+        for t in range(PACK):
+            nc.vector.scalar_tensor_tensor(
+                hm[t][:, 0:V], both[:, planes[t]], unit_sb[:, t : t + 1], gain[:, planes[t]], ALU.mult, ALU.mult
+            )
+
+        hid = [sb("hid%d" % u, [P, 2, U], F32) for u in range(2)]
+        woven = sb("woven", [P, U * PACK], BF16)
+        woven3 = woven[:].rearrange("p (n t) -> p n t", t=PACK)
+        for t in range(PACK - 1):
+            nc.vector.tensor_copy(hid[t // 2][:, t % 2, :], hm[t][:].indirect(own_sb[:]))
+            if t == 1:
+                nc.scalar.copy(woven3[:, :, 0:2], hid[0][:].rearrange("p t n -> p n t"))
+        chunks = [slice(c, c + CHUNK) for c in range(0, U, CHUNK)]
+        for c in chunks:
+            nc.vector.tensor_copy(hid[1][:, 1, c], hm[PACK - 1][:].indirect(own_sb[:, c.start // 16 : c.stop // 16]))
+            nc.scalar.copy(woven3[:, c, 2:4], hid[1][:, :, c].rearrange("p t n -> p n t"))
+
+        out3 = out.rearrange("(h p) c -> p h c", p=P)
+        accs = []
+        for i, c in enumerate(chunks):
+            hq = sb("hq%d" % i, [P, CHUNK], U32)
+            hs = sb("hs%d" % i, [P, CHUNK], U8)
+            nc.vector.quantize_mx(hq[:].bitcast(FP8X4), hs[:], woven[:, PACK * c.start : PACK * c.stop])
+            acc = psum.tile([P, N // P, CHUNK], F32, name="r_ps%d" % i, tag="bank%d" % i)
+            for h in range(N // P):
+                nc.tensor.matmul_mx(
+                    acc[:, h, :],
+                    lhsT=w2w[:, 2 * P * h : 2 * P * (h + 1)].bitcast(FP4X4),
+                    lhsT_scale=w2s[:, P * h : P * (h + 1)],
+                    rhs=hq[:].bitcast(FP8X4),
+                    rhs_scale=hs[:],
+                    start=True,
+                    stop=True,
+                )
+            accs.append(acc)
+        for i, c in enumerate(chunks):
+            res = sb("res%d" % i, [P, N // P, CHUNK], F32)
+            nc.vector.tensor_tensor(res[:], accs[i][:], skip_sb[:, :, c], ALU.add)
+            nc.sync.dma_start(out3[:, :, c], res[:])

@@ -1,6 +1,7 @@
 from contextlib import ExitStack
 
 import concourse.mybir as mybir
+from concourse.masks import make_identity
 
 F32 = mybir.dt.float32
 BF16 = mybir.dt.bfloat16
@@ -18,7 +19,7 @@ PACK = 4
 T, S, N, H, V, U = 1024, 512, 256, 512, 256, 512
 HALF = S // 2
 CHUNK = 128
-WIDE = 704
+WIDE = 512
 
 FLOPS = 2 * 512 * H * S + 2 * H * N * U
 
@@ -31,8 +32,8 @@ def tile_picked_ytomeg_mul_p_kernel(
         keep = ctx.enter_context(tc.tile_pool(name="keep", bufs=1))
         psum = ctx.enter_context(tc.psum_pool(name="psum", bufs=1))
 
-        def sb(name, shape, dtype):
-            return keep.tile(shape, dtype, name=name, align_bytes=64)
+        def sb(name, shape, dtype, tag=""):
+            return keep.tile(shape, dtype, name=name, tag=tag or name, align_bytes=64)
 
         offs_sb = sb("offs_sb", [P, S // 16], U16)
         dst_sb = sb("dst_sb", [P, V // 16], U16)
@@ -42,119 +43,164 @@ def tile_picked_ytomeg_mul_p_kernel(
         xs = sb("xs", [P, T], U8)
         w1w = sb("w1w", [P, 2 * H], U8)
         w1s = sb("w1s", [P, H], U8)
-        w2w = sb("w2w", [P, 2 * N], U8)
-        w2s = sb("w2s", [P, N], U8)
         sza_sb = sb("sza_sb", [P, PACK * V], F32)
         szb_sb = sb("szb_sb", [P, PACK * V], F32)
         unit_sb = sb("unit_sb", [P, PACK], F32)
-        skip_sb = sb("skip_sb", [P, N // P, U], F32)
 
         def load_scales(plane, rows, queues):
             for q in range(4):
                 queues[q].dma_start(
-                    plane[32 * q : 32 * q + 4, :].bitcast(I32), rows[0, 4 * q : 4 * q + 4, :].bitcast(I32)
+                    plane[32 * q : 32 * q + 4, 0 : rows.shape[2]].bitcast(I32), rows[0, 4 * q : 4 * q + 4, :].bitcast(I32)
                 )
 
         nc.vector.memset(xs[:].bitcast(I32), 0)
         nc.vector.memset(w1s[:].bitcast(I32), 0)
-        nc.vector.memset(w2s[:].bitcast(I32), 0)
         nc.sync.dma_start(offs_sb[:], offs)
-        nc.scalar.dma_start(xw[:].bitcast(I32), x_words[0].rearrange("p n t -> p (n t)").bitcast(I32))
-        nc.gpsimd.dma_start(sza_sb[:], sza.rearrange("(p t) v -> p (t v)", t=PACK))
-        nc.gpsimd.dma_start(szb_sb[:], szb.rearrange("(p t) v -> p (t v)", t=PACK))
+        nc.scalar.dma_start(w1w[:].bitcast(I32), w1_words[0].bitcast(I32))
         load_scales(xs, x_scales, [nc.sync, nc.scalar, nc.sync, nc.scalar])
-        nc.sync.dma_start(w1w[:].bitcast(I32), w1_words[0].bitcast(I32))
-        load_scales(w1s, w1_scales, [nc.scalar, nc.sync, nc.sync, nc.sync])
+        nc.sync.dma_start(xw[:].bitcast(I32), x_words[0].rearrange("p n t -> p (n t)").bitcast(I32))
+        load_scales(w1s, w1_scales, [nc.scalar, nc.sync, nc.scalar, nc.sync])
         nc.sync.dma_start(src_sb[:], src)
+        nc.sync.dma_start(sza_sb[:], sza.rearrange("(p t) v -> p (t v)", t=PACK))
+        nc.sync.dma_start(szb_sb[:], szb.rearrange("(p t) v -> p (t v)", t=PACK))
         nc.sync.dma_start(dst_sb[:], dst)
-        nc.sync.dma_start(unit_sb[:], unit.rearrange("(p t) o -> p (t o)", t=PACK))
         nc.sync.dma_start(own_sb[:], own)
-        nc.sync.dma_start(w2w[:].bitcast(I32), w2_words[0].bitcast(I32))
-        load_scales(w2s, w2_scales, [nc.sync] * 4)
-        nc.sync.dma_start(skip_sb[:], skip.rearrange("(h p) c -> p h c", p=P))
+        nc.sync.dma_start(unit_sb[:], unit.rearrange("(p t) o -> p (t o)", t=PACK))
 
         warm = sb("warm", [P, 2], F32)
-        nc.gpsimd.memset(warm[:, 0:1], 1.0)
+        nc.vector.memset(warm[:, 0:1], 1.0)
         nc.scalar.activation(warm[:, 1:2], warm[:, 0:1], ACT.Abs_reciprocal_sqrt)
 
-        hm = [sb("hm%d" % t, [P, WIDE if t < PACK - 1 else V], F32) for t in range(PACK)]
-        for t in range(PACK - 1):
-            nc.gpsimd.memset(hm[t][:, V:], 0.0)
+        ident = sb("ident", [P, P], F32)
+        nc.vector.memset(ident[:], 0.0)
+        make_identity(nc, ident[:], nomemset=True)
+        hm = [sb("hm%d" % t, [P, WIDE if t < 2 else V], F32) for t in range(PACK)]
+        for t in range(2):
+            nc.vector.memset(hm[t][:, V:], 0.0)
 
-        w1wd = sb("w1wd", [P, 2 * H], U8)
-        w1sd = sb("w1sd", [P, H], U8)
-        nc.vector.tensor_copy(
-            w1wd[:].rearrange("p (t m b) -> p t m b", t=PACK, b=2),
-            w1w[:].rearrange("p (m t b) -> p t m b", t=PACK, b=2),
-        )
+        w1w4 = w1w[:].rearrange("p (m t b) -> p t m b", t=PACK, b=2)
+        w1s3 = w1s[:].rearrange("p (m t) -> p t m", t=PACK)
+        early_words = sb("early_words", [P, 4 * P], U8)
+        nc.vector.tensor_copy(early_words[:].rearrange("p (t m b) -> p t m b", t=2, b=2), w1w4[:, 0:2])
 
-        xqw = [sb("xqw%d" % h, [P, HALF], U32) for h in range(2)]
-        xqs = [sb("xqs%d" % h, [P, HALF], U8) for h in range(2)]
+        xqs = sb("xqs", [P, S], U8)
         y = [sb("y%d" % t, [P, S], F32) for t in range(PACK)]
-        for h in range(2):
-            piece = offs_sb[:, h * (HALF // 16) : (h + 1) * (HALF // 16)]
-            nc.vector.tensor_copy(xqs[h][:], xs[:].indirect(piece))
-            if h == 0:
-                nc.gpsimd.tensor_copy(
-                    w1sd[:].rearrange("p (t m) -> p t m", t=PACK), w1s[:].rearrange("p (m t) -> p t m", t=PACK)
-                )
-            nc.vector.tensor_copy(xqw[h][:], xw[:].indirect(piece))
-            for t in range(PACK):
-                acc = psum.tile([P, HALF], F32, name="y_ps%d_%d" % (h, t), tag="bank%d" % (PACK * h + t))
+        nc.vector.tensor_copy(xqs[:], xs[:].indirect(offs_sb[:]))
+        xqw = [sb("xqw0", [P, HALF], U32)]
+        nc.vector.tensor_copy(xqw[0][:], xw[:].indirect(offs_sb[:, 0 : HALF // 16]))
+        w1sd = sb("w1sd", [P, H], U8)
+        nc.vector.tensor_copy(w1sd[:].rearrange("p (t m) -> p t m", t=PACK), w1s3)
+        xqw.append(sb("xqw1", [P, HALF], U32, tag="w1s"))
+        nc.vector.tensor_copy(xqw[1][:], xw[:].indirect(offs_sb[:, HALF // 16 :]))
+        late_words = sb("late_words", [P, 4 * P], U8, tag="xw")
+        nc.vector.tensor_copy(late_words[:].rearrange("p (t m b) -> p t m b", t=2, b=2), w1w4[:, 2:4])
+        w1wd = [words[:, 2 * P * j : 2 * P * (j + 1)] for words in (early_words, late_words) for j in range(2)]
+
+        def bank(name, b, shape):
+            return psum.tile(shape, F32, name=name, tag="bank%d" % b)
+
+        for t in range(PACK):
+            for h in range(2):
+                acc = bank("y_ps%d_%d" % (t, h), 2 * t + h, [P, HALF])
                 nc.tensor.matmul_mx(
                     acc[:],
-                    lhsT=w1wd[:, 2 * P * t : 2 * P * (t + 1)].bitcast(FP4X4),
+                    lhsT=w1wd[t].bitcast(FP4X4),
                     lhsT_scale=w1sd[:, P * t : P * (t + 1)],
                     rhs=xqw[h][:].bitcast(FP8X4),
-                    rhs_scale=xqs[h][:],
+                    rhs_scale=xqs[:, h * HALF : (h + 1) * HALF],
                     start=True,
                     stop=True,
                 )
                 nc.scalar.copy(y[t][:, h * HALF : (h + 1) * HALF], acc[:])
 
-        sz = sb("sz", [P, PACK * V], F32)
-        root = sb("root", [P, PACK * V], F32)
-        inv = sb("inv", [P, PACK * V], F32)
-        sgn = sb("sgn", [P, PACK * V], F32)
-        rcp = sb("rcp", [P, PACK * V], F32)
-        pairs = [slice(0, 2 * V), slice(2 * V, 4 * V)]
-        nc.vector.tensor_tensor(sz[:], sza_sb[:], szb_sb[:], ALU.add)
-        nc.scalar.activation(root[:], sz[:], ACT.Abs_reciprocal_sqrt)
-        nc.scalar.activation(inv[:], root[:], ACT.Square)
-        nc.scalar.activation(sgn[:], sz[:], ACT.Sign)
+        w2w = sb("w2w", [P, 2 * N], U8, tag="w1w")
+        nc.sync.dma_start(w2w[:].bitcast(I32), w2_words[0].bitcast(I32))
+        w2s = w1sd
+        load_scales(w2s, w2_scales, [nc.sync] * 4)
 
-        yr = sb("yr", [P, PACK * V], F32)
-        kept = sb("kept", [P, PACK * V], F32)
-        merged = sb("merged", [P, PACK * V], F32)
-        th = sb("th", [P, PACK * V], F32)
-        both = sb("both", [P, PACK * V], F32)
-        gain = sb("gain", [P, PACK * V], F32)
+        PAIR = 2 * V
+
+        def turn(name, b, terms):
+            width = terms[0].shape[1]
+            acc = bank(name, b, [P, width])
+            for j in range(width // P):
+                for i, term in enumerate(terms):
+                    nc.tensor.matmul(
+                        acc[:, j * P : (j + 1) * P],
+                        lhsT=term[:, j * P : (j + 1) * P],
+                        rhs=ident[:],
+                        is_transpose=True,
+                        start=(i == 0),
+                        stop=(i == len(terms) - 1),
+                    )
+            return acc
+
+        def halves(name):
+            return [sb("%s%d" % (name, u), [P, PAIR], F32) for u in range(2)]
+
+        root, kept = halves("root"), halves("kept")
+        th = [root[1], root[0]]
+        inv = sb("inv", [P, 2 * PAIR], F32)
+        sgn = sb("sgn", [P, 2 * PAIR], F32)
+        yr = sb("yr", [P, 2 * PAIR], F32)
+        merged = sb("merged", [P, 2 * PAIR], F32)
+        pairs = [slice(0, PAIR), slice(PAIR, 2 * PAIR)]
         planes = [slice(t * V, (t + 1) * V) for t in range(PACK)]
+
+        for u in range(2):
+            sz_t = turn("sz_t%d" % u, 6 + u, [sza_sb[:, pairs[u]], szb_sb[:, pairs[u]]])
+            nc.scalar.activation(root[u][:], sz_t[:], ACT.Abs_reciprocal_sqrt)
+            nc.scalar.activation(sgn[:, pairs[u]], sz_t[:], ACT.Sign)
+            nc.scalar.activation(inv[:, pairs[u]], root[u][:], ACT.Square)
         for t in range(PACK):
             nc.vector.tensor_copy(yr[:, planes[t]], y[t][:].indirect(src_sb[:]))
-        for t in range(PACK):
-            nc.vector.tensor_tensor(kept[:, planes[t]], y[t][:].indirect(dst_sb[:]), sza_sb[:, planes[t]], ALU.mult)
-        nc.scalar.activation(th[:], yr[:], ACT.Tanh)
-        nc.vector.tensor_tensor(merged[:], yr[:], szb_sb[:], ALU.mult)
-        nc.vector.tensor_tensor(rcp[:], inv[:], sgn[:], ALU.mult)
-        nc.vector.tensor_tensor(both[:], kept[:], merged[:], ALU.add)
-        nc.vector.tensor_tensor(gain[:], th[:], rcp[:], ALU.mult)
-        for t in range(PACK):
+        for u in range(2):
+            nc.scalar.activation(th[u][:], yr[:, pairs[u]], ACT.Tanh)
+        for c in pairs:
+            nc.vector.tensor_tensor(merged[:, c], yr[:, c], szb_sb[:, c], ALU.mult)
+        both_t = []
+        for u in range(2):
+            for j in range(2):
+                t = 2 * u + j
+                nc.vector.tensor_tensor(
+                    kept[u][:, planes[j]], y[t][:].indirect(dst_sb[:]), sza_sb[:, planes[t]], ALU.mult
+                )
+            both_t.append(turn("both_t%d" % u, 6 + u, [kept[u][:], merged[:, pairs[u]]]))
+        skip_sb = sb("skip_sb", [P, N // P, U], F32, tag="sza_sb")
+        nc.sync.dma_start(skip_sb[:], skip.rearrange("(h p) c -> p h c", p=P))
+        rcp = sb("rcp", [P, 2 * PAIR], F32, tag="y3")
+        for c in pairs:
+            nc.vector.tensor_tensor(rcp[:, c], inv[:, c], sgn[:, c], ALU.mult)
+        mrg_t = sb("mrg_t", [P, 2 * PAIR], F32, tag="sgn")
+        mrg = []
+        for u in range(2):
+            nc.vector.tensor_tensor(mrg_t[:, pairs[u]], both_t[u][:], rcp[:, pairs[u]], ALU.mult)
+            for j in range(2):
+                mrg.append(turn("mrg%d" % (2 * u + j), 2 * u + j, [mrg_t[:, planes[2 * u + j]]]))
+
+        def gate(t):
             nc.vector.scalar_tensor_tensor(
-                hm[t][:, 0:V], both[:, planes[t]], unit_sb[:, t : t + 1], gain[:, planes[t]], ALU.mult, ALU.mult
+                hm[t][:, 0:V], mrg[t][:], unit_sb[:, t : t + 1], th[t // 2][:, planes[t % 2]], ALU.mult, ALU.mult
             )
 
-        hid = [sb("hid%d" % u, [P, 2, U], F32) for u in range(2)]
         woven = sb("woven", [P, U * PACK], BF16)
         woven3 = woven[:].rearrange("p (n t) -> p n t", t=PACK)
-        for t in range(PACK - 1):
-            nc.vector.tensor_copy(hid[t // 2][:, t % 2, :], hm[t][:].indirect(own_sb[:]))
-            if t == 1:
-                nc.scalar.copy(woven3[:, :, 0:2], hid[0][:].rearrange("p t n -> p n t"))
+
+        def unmerge(u, c):
+            hid = sb("hid%d_%d" % (u, c.start), [P, 2, c.stop - c.start], F32)
+            for j in range(2):
+                nc.vector.tensor_copy(hid[:, j, :], hm[2 * u + j][:].indirect(own_sb[:, c.start // 16 : c.stop // 16]))
+            nc.scalar.copy(woven3[:, c, 2 * u : 2 * u + 2], hid[:].rearrange("p t n -> p n t"))
+
         chunks = [slice(c, c + CHUNK) for c in range(0, U, CHUNK)]
+        gate(0)
+        gate(1)
+        unmerge(0, slice(0, U // 2))
+        gate(2)
+        gate(3)
+        unmerge(0, slice(U // 2, U))
         for c in chunks:
-            nc.vector.tensor_copy(hid[1][:, 1, c], hm[PACK - 1][:].indirect(own_sb[:, c.start // 16 : c.stop // 16]))
-            nc.scalar.copy(woven3[:, c, 2:4], hid[1][:, :, c].rearrange("p t n -> p n t"))
+            unmerge(1, c)
 
         out3 = out.rearrange("(h p) c -> p h c", p=P)
         accs = []
@@ -162,7 +208,7 @@ def tile_picked_ytomeg_mul_p_kernel(
             hq = sb("hq%d" % i, [P, CHUNK], U32)
             hs = sb("hs%d" % i, [P, CHUNK], U8)
             nc.vector.quantize_mx(hq[:].bitcast(FP8X4), hs[:], woven[:, PACK * c.start : PACK * c.stop])
-            acc = psum.tile([P, N // P, CHUNK], F32, name="r_ps%d" % i, tag="bank%d" % i)
+            acc = bank("r_ps%d" % i, 4 + i, [P, N // P, CHUNK])
             for h in range(N // P):
                 nc.tensor.matmul_mx(
                     acc[:, h, :],
@@ -174,7 +220,9 @@ def tile_picked_ytomeg_mul_p_kernel(
                     stop=True,
                 )
             accs.append(acc)
+        first = sb("first", [P, N // P, CHUNK], F32)
+        rest = sb("rest", [P, len(chunks) - 1, N // P, CHUNK], F32, tag="woven")
         for i, c in enumerate(chunks):
-            res = sb("res%d" % i, [P, N // P, CHUNK], F32)
-            nc.vector.tensor_tensor(res[:], accs[i][:], skip_sb[:, :, c], ALU.add)
-            nc.sync.dma_start(out3[:, :, c], res[:])
+            res = first[:] if i == 0 else rest[:, i - 1]
+            nc.vector.tensor_tensor(res, accs[i][:], skip_sb[:, :, c], ALU.add)
+            nc.sync.dma_start(out3[:, :, c], res)

@@ -101,7 +101,7 @@ def tile_picked_ytomeg_mul_p_kernel(
 
         for t in range(PACK):
             for h in range(2):
-                acc = bank("y_ps%d_%d" % (t, h), 2 * t + h, [P, HALF])
+                acc = bank("y_ps%d_%d" % (t, h), 0 if (t, h) == (1, 0) else 2 * t + h, [P, HALF])
                 nc.tensor.matmul_mx(
                     acc[:],
                     lhsT=w1wd[t].bitcast(FP4X4),
@@ -175,12 +175,11 @@ def tile_picked_ytomeg_mul_p_kernel(
         mrg = []
         for u in range(2):
             nc.vector.tensor_tensor(mrg_t[:, pairs[u]], both_t[u][:], rcp[:, pairs[u]], ALU.mult)
-            for j in range(2):
-                mrg.append(turn("mrg%d" % (2 * u + j), 2 * u + j, [mrg_t[:, planes[2 * u + j]]]))
+            mrg.append(turn("mrg%d" % u, u, [mrg_t[:, pairs[u]]]))
 
         def gate(t):
             nc.vector.scalar_tensor_tensor(
-                hm[t][:, 0:V], mrg[t][:], unit_sb[:, t : t + 1], th[t // 2][:, planes[t % 2]], ALU.mult, ALU.mult
+                hm[t][:, 0:V], mrg[t // 2][:, planes[t % 2]], unit_sb[:, t : t + 1], th[t // 2][:, planes[t % 2]], ALU.mult, ALU.mult
             )
 
         woven = sb("woven", [P, U * PACK], BF16)

from contextlib import ExitStack

import concourse.mybir as mybir
from concourse.masks import make_identity

F32 = mybir.dt.float32
BF16 = mybir.dt.bfloat16
I32 = mybir.dt.int32
U32 = mybir.dt.uint32
U16 = mybir.dt.uint16
U8 = mybir.dt.uint8
FP8X4 = mybir.dt.float8_e4m3fn_x4
FP4X4 = mybir.dt.float4_e2m1fn_x4
ALU = mybir.AluOpType
ACT = mybir.ActivationFunctionType

P = 128
PACK = 4
T, S, N, H, V, U = 1024, 512, 256, 512, 256, 512
HALF = S // 2
CHUNK = 128
WIDE = 512

FLOPS = 2 * 512 * H * S + 2 * H * N * U


def tile_picked_ytomeg_mul_p_kernel(
    tc, x_words, x_scales, w1_words, w1_scales, sza, szb, unit, w2_words, w2_scales, skip, offs, dst, src, own, out
):
    nc = tc.nc
    with ExitStack() as ctx:
        keep = ctx.enter_context(tc.tile_pool(name="keep", bufs=1))
        psum = ctx.enter_context(tc.psum_pool(name="psum", bufs=1))

        def sb(name, shape, dtype, tag=""):
            return keep.tile(shape, dtype, name=name, tag=tag or name, align_bytes=64)

        offs_sb = sb("offs_sb", [P, S // 16], U16)
        dst_sb = sb("dst_sb", [P, V // 16], U16)
        src_sb = sb("src_sb", [P, V // 16], U16)
        own_sb = sb("own_sb", [P, U // 16], U16)
        xw = sb("xw", [P, T], U32)
        xs = sb("xs", [P, T], U8)
        w1w = sb("w1w", [P, 2 * H], U8)
        w1s = sb("w1s", [P, H], U8)
        sza_sb = sb("sza_sb", [P, PACK * V], F32)
        szb_sb = sb("szb_sb", [P, PACK * V], F32)
        unit_sb = sb("unit_sb", [P, PACK], F32)

        def load_scales(plane, rows, queues):
            for q in range(4):
                queues[q].dma_start(
                    plane[32 * q : 32 * q + 4, 0 : rows.shape[2]].bitcast(I32), rows[0, 4 * q : 4 * q + 4, :].bitcast(I32)
                )

        nc.vector.memset(xs[:].bitcast(I32), 0)
        nc.vector.memset(w1s[:].bitcast(I32), 0)
        nc.sync.dma_start(offs_sb[:], offs)
        nc.scalar.dma_start(w1w[:].bitcast(I32), w1_words[0].bitcast(I32))
        load_scales(xs, x_scales, [nc.sync, nc.scalar, nc.sync, nc.scalar])
        nc.sync.dma_start(xw[:].bitcast(I32), x_words[0].rearrange("p n t -> p (n t)").bitcast(I32))
        load_scales(w1s, w1_scales, [nc.scalar, nc.sync, nc.scalar, nc.sync])
        nc.sync.dma_start(src_sb[:], src)
        nc.sync.dma_start(sza_sb[:], sza.rearrange("(p t) v -> p (t v)", t=PACK))
        nc.sync.dma_start(szb_sb[:], szb.rearrange("(p t) v -> p (t v)", t=PACK))
        nc.sync.dma_start(dst_sb[:], dst)
        nc.sync.dma_start(own_sb[:], own)
        nc.sync.dma_start(unit_sb[:], unit.rearrange("(p t) o -> p (t o)", t=PACK))

        warm = sb("warm", [P, 2], F32)
        nc.vector.memset(warm[:, 0:1], 1.0)
        nc.scalar.activation(warm[:, 1:2], warm[:, 0:1], ACT.Abs_reciprocal_sqrt)

        ident = sb("ident", [P, P], F32)
        nc.vector.memset(ident[:], 0.0)
        make_identity(nc, ident[:], nomemset=True)
        hm = [sb("hm%d" % t, [P, WIDE if t < 2 else V], F32) for t in range(PACK)]
        for t in range(2):
            nc.vector.memset(hm[t][:, V:], 0.0)

        w1w4 = w1w[:].rearrange("p (m t b) -> p t m b", t=PACK, b=2)
        w1s3 = w1s[:].rearrange("p (m t) -> p t m", t=PACK)
        early_words = sb("early_words", [P, 4 * P], U8)
        nc.vector.tensor_copy(early_words[:].rearrange("p (t m b) -> p t m b", t=2, b=2), w1w4[:, 0:2])

        xqs = sb("xqs", [P, S], U8)
        y = [sb("y%d" % t, [P, S], F32) for t in range(PACK)]
        nc.vector.tensor_copy(xqs[:], xs[:].indirect(offs_sb[:]))
        xqw = [sb("xqw0", [P, HALF], U32)]
        nc.vector.tensor_copy(xqw[0][:], xw[:].indirect(offs_sb[:, 0 : HALF // 16]))
        w1sd = sb("w1sd", [P, H], U8)
        nc.vector.tensor_copy(w1sd[:].rearrange("p (t m) -> p t m", t=PACK), w1s3)
        xqw.append(sb("xqw1", [P, HALF], U32, tag="w1s"))
        nc.vector.tensor_copy(xqw[1][:], xw[:].indirect(offs_sb[:, HALF // 16 :]))
        late_words = sb("late_words", [P, 4 * P], U8, tag="xw")
        nc.vector.tensor_copy(late_words[:].rearrange("p (t m b) -> p t m b", t=2, b=2), w1w4[:, 2:4])
        w1wd = [words[:, 2 * P * j : 2 * P * (j + 1)] for words in (early_words, late_words) for j in range(2)]

        def bank(name, b, shape):
            return psum.tile(shape, F32, name=name, tag="bank%d" % b)

        for t in range(PACK):
            for h in range(2):
                acc = bank("y_ps%d_%d" % (t, h), 0 if (t, h) == (1, 0) else 2 * t + h, [P, HALF])
                nc.tensor.matmul_mx(
                    acc[:],
                    lhsT=w1wd[t].bitcast(FP4X4),
                    lhsT_scale=w1sd[:, P * t : P * (t + 1)],
                    rhs=xqw[h][:].bitcast(FP8X4),
                    rhs_scale=xqs[:, h * HALF : (h + 1) * HALF],
                    start=True,
                    stop=True,
                )
                nc.scalar.copy(y[t][:, h * HALF : (h + 1) * HALF], acc[:])

        w2w = sb("w2w", [P, 2 * N], U8, tag="w1w")
        nc.sync.dma_start(w2w[:].bitcast(I32), w2_words[0].bitcast(I32))
        w2s = w1sd
        load_scales(w2s, w2_scales, [nc.sync] * 4)

        PAIR = 2 * V

        def turn(name, b, terms):
            width = terms[0].shape[1]
            acc = bank(name, b, [P, width])
            for j in range(width // P):
                for i, term in enumerate(terms):
                    nc.tensor.matmul(
                        acc[:, j * P : (j + 1) * P],
                        lhsT=term[:, j * P : (j + 1) * P],
                        rhs=ident[:],
                        is_transpose=True,
                        start=(i == 0),
                        stop=(i == len(terms) - 1),
                    )
            return acc

        def halves(name):
            return [sb("%s%d" % (name, u), [P, PAIR], F32) for u in range(2)]

        root, kept = halves("root"), halves("kept")
        th = [root[1], root[0]]
        inv = sb("inv", [P, 2 * PAIR], F32)
        sgn = sb("sgn", [P, 2 * PAIR], F32)
        yr = sb("yr", [P, 2 * PAIR], F32)
        merged = sb("merged", [P, 2 * PAIR], F32)
        pairs = [slice(0, PAIR), slice(PAIR, 2 * PAIR)]
        planes = [slice(t * V, (t + 1) * V) for t in range(PACK)]

        for u in range(2):
            sz_t = turn("sz_t%d" % u, 6 + u, [sza_sb[:, pairs[u]], szb_sb[:, pairs[u]]])
            nc.scalar.activation(root[u][:], sz_t[:], ACT.Abs_reciprocal_sqrt)
            nc.scalar.activation(sgn[:, pairs[u]], sz_t[:], ACT.Sign)
            nc.scalar.activation(inv[:, pairs[u]], root[u][:], ACT.Square)
        for t in range(PACK):
            nc.vector.tensor_copy(yr[:, planes[t]], y[t][:].indirect(src_sb[:]))
        for u in range(2):
            nc.scalar.activation(th[u][:], yr[:, pairs[u]], ACT.Tanh)
        for c in pairs:
            nc.vector.tensor_tensor(merged[:, c], yr[:, c], szb_sb[:, c], ALU.mult)
        both_t = []
        for u in range(2):
            for j in range(2):
                t = 2 * u + j
                nc.vector.tensor_tensor(
                    kept[u][:, planes[j]], y[t][:].indirect(dst_sb[:]), sza_sb[:, planes[t]], ALU.mult
                )
            both_t.append(turn("both_t%d" % u, 6 + u, [kept[u][:], merged[:, pairs[u]]]))
        skip_sb = sb("skip_sb", [P, N // P, U], F32, tag="sza_sb")
        nc.sync.dma_start(skip_sb[:], skip.rearrange("(h p) c -> p h c", p=P))
        rcp = sb("rcp", [P, 2 * PAIR], F32, tag="y3")
        for c in pairs:
            nc.vector.tensor_tensor(rcp[:, c], inv[:, c], sgn[:, c], ALU.mult)
        mrg_t = sb("mrg_t", [P, 2 * PAIR], F32, tag="sgn")
        mrg = []
        for u in range(2):
            nc.vector.tensor_tensor(mrg_t[:, pairs[u]], both_t[u][:], rcp[:, pairs[u]], ALU.mult)
            mrg.append(turn("mrg%d" % u, u, [mrg_t[:, pairs[u]]]))

        def gate(t):
            nc.vector.scalar_tensor_tensor(
                hm[t][:, 0:V], mrg[t // 2][:, planes[t % 2]], unit_sb[:, t : t + 1], th[t // 2][:, planes[t % 2]], ALU.mult, ALU.mult
            )

        woven = sb("woven", [P, U * PACK], BF16)
        woven3 = woven[:].rearrange("p (n t) -> p n t", t=PACK)

        def unmerge(u, c):
            hid = sb("hid%d_%d" % (u, c.start), [P, 2, c.stop - c.start], F32)
            for j in range(2):
                nc.vector.tensor_copy(hid[:, j, :], hm[2 * u + j][:].indirect(own_sb[:, c.start // 16 : c.stop // 16]))
            nc.scalar.copy(woven3[:, c, 2 * u : 2 * u + 2], hid[:].rearrange("p t n -> p n t"))

        chunks = [slice(c, c + CHUNK) for c in range(0, U, CHUNK)]
        gate(0)
        gate(1)
        unmerge(0, slice(0, U // 2))
        gate(2)
        gate(3)
        unmerge(0, slice(U // 2, U))
        for c in chunks:
            unmerge(1, c)

        out3 = out.rearrange("(h p) c -> p h c", p=P)
        accs = []
        for i, c in enumerate(chunks):
            hq = sb("hq%d" % i, [P, CHUNK], U32)
            hs = sb("hs%d" % i, [P, CHUNK], U8)
            nc.vector.quantize_mx(hq[:].bitcast(FP8X4), hs[:], woven[:, PACK * c.start : PACK * c.stop])
            acc = bank("r_ps%d" % i, 4 + i, [P, N // P, CHUNK])
            for h in range(N // P):
                nc.tensor.matmul_mx(
                    acc[:, h, :],
                    lhsT=w2w[:, 2 * P * h : 2 * P * (h + 1)].bitcast(FP4X4),
                    lhsT_scale=w2s[:, P * h : P * (h + 1)],
                    rhs=hq[:].bitcast(FP8X4),
                    rhs_scale=hs[:],
                    start=True,
                    stop=True,
                )
            accs.append(acc)
        first = sb("first", [P, N // P, CHUNK], F32)
        rest = sb("rest", [P, len(chunks) - 1, N // P, CHUNK], F32, tag="woven")
        for i, c in enumerate(chunks):
            res = first[:] if i == 0 else rest[:, i - 1]
            nc.vector.tensor_tensor(res, accs[i][:], skip_sb[:, :, c], ALU.add)
            nc.sync.dma_start(out3[:, :, c], res)
